import numpy as np
CORES = [56,57,58,59,60,61,62,63,184,185,186,187,188,189,190,191]
N = 16
def setup_inputs(rng):
    return {"x": rng.standard_normal((N, 128, 64), dtype=np.float32)}
def reference(x):
    g = np.concatenate(list(x), axis=1)
    return {"y": np.broadcast_to(g, (N,) + g.shape)}

@@ -1,0 +1,59 @@
+from concourse.bass import DstId, RemoteDMATransfer
+
+SCRATCH = {
+    "land": ("sbuf", [128, 1024], "float32"),
+}
+SEMAPHORES = ["loaded", "sent", "near", "peer", "far", "stored"]
+
+W = 64
+
+
+def rank_program(g, core, T, topo):
+    rank = T.rank_of(core)
+    if rank is None:
+        return
+    cores = list(T.cores)
+    mates = [c for c in cores if c != core and topo.host(c) == topo.host(core)]
+    peer = [c for c in cores if topo.host(c) != topo.host(core) and c % 8 == core % 8][0]
+    prank = T.rank_of(peer)
+
+    def ids(dsts):
+        out = []
+        for d in dsts:
+            rid, pid = topo.addr(d, core)
+            out.append(DstId(rid=rid, pnc=pid))
+        return out
+
+    mine = T.land[:, rank * W:(rank + 1) * W]
+    theirs = T.land[:, prank * W:(prank + 1) * W]
+
+    g.dma_start(mine, T.x[:]).then_inc(T.sem.loaded, 16)
+    g.wait_ge(T.sem.loaded, 16)
+
+    g.remote_dma_fused(
+        [
+            RemoteDMATransfer(dst_ids=ids([peer]), dma_engine_mask=0x00FF, remote_sem=T.sem.peer,
+                              srcs=[mine], dsts=[mine]),
+            RemoteDMATransfer(dst_ids=ids(mates), dma_engine_mask=0xFF00, remote_sem=T.sem.near,
+                              srcs=[mine], dsts=[mine] * 7),
+        ],
+        local_sem=T.sem.sent,
+    )
+
+    g.wait_ge(T.sem.peer, 8)
+    g.remote_dma_fused(
+        [
+            RemoteDMATransfer(dst_ids=ids(mates), dma_engine_mask=0xFFFF, remote_sem=T.sem.far,
+                              srcs=[theirs], dsts=[theirs] * 7),
+        ],
+        local_sem=T.sem.sent,
+    )
+
+    h0 = (rank // 8) * 512
+    p0 = (prank // 8) * 512
+    g.wait_ge(T.sem.near, 7 * 8)
+    g.dma_start(T.y[:, h0:h0 + 512], T.land[:, h0:h0 + 512]).then_inc(T.sem.stored, 16)
+    g.wait_ge(T.sem.far, 7 * 16)
+    g.dma_start(T.y[:, p0:p0 + 512], T.land[:, p0:p0 + 512]).then_inc(T.sem.stored, 16)
+    g.wait_ge(T.sem.sent, 32)
+    g.wait_ge(T.sem.stored, 32)

@@ -14,6 +14,8 @@ def rank_program(g, core, T, topo):
         return
     cores = list(T.cores)
     mates = [c for c in cores if c != core and topo.host(c) == topo.host(core)]
+    same_die = [c for c in mates if topo.die(c) == topo.die(core)]
+    other_die = [c for c in mates if topo.die(c) != topo.die(core)]
     peer = [c for c in cores if topo.host(c) != topo.host(core) and c % 8 == core % 8][0]
     prank = T.rank_of(peer)
 
@@ -34,8 +36,15 @@ def rank_program(g, core, T, topo):
         [
             RemoteDMATransfer(dst_ids=ids([peer]), dma_engine_mask=0x00FF, remote_sem=T.sem.peer,
                               srcs=[mine], dsts=[mine]),
-            RemoteDMATransfer(dst_ids=ids(mates), dma_engine_mask=0xFF00, remote_sem=T.sem.near,
-                              srcs=[mine], dsts=[mine] * 7),
+            RemoteDMATransfer(dst_ids=ids(other_die), dma_engine_mask=0xFF00, remote_sem=T.sem.near,
+                              srcs=[mine], dsts=[mine] * 4),
+        ],
+        local_sem=T.sem.sent,
+    )
+    g.remote_dma_fused(
+        [
+            RemoteDMATransfer(dst_ids=ids(same_die), dma_engine_mask=0x00FF, remote_sem=T.sem.near,
+                              srcs=[mine], dsts=[mine] * 3),
         ],
         local_sem=T.sem.sent,
     )
@@ -50,10 +59,10 @@ def rank_program(g, core, T, topo):
     )
 
     h0 = (rank // 8) * 512
-    p0 = (prank // 8) * 512
+    p0 = 512 - h0
     g.wait_ge(T.sem.near, 7 * 8)
     g.dma_start(T.y[:, h0:h0 + 512], T.land[:, h0:h0 + 512]).then_inc(T.sem.stored, 16)
     g.wait_ge(T.sem.far, 7 * 16)
     g.dma_start(T.y[:, p0:p0 + 512], T.land[:, p0:p0 + 512]).then_inc(T.sem.stored, 16)
-    g.wait_ge(T.sem.sent, 32)
+    g.wait_ge(T.sem.sent, 16 + 8 + 16)
     g.wait_ge(T.sem.stored, 32)

@@ -13,9 +13,10 @@ def rank_program(g, core, T, topo):
     if rank is None:
         return
     cores = list(T.cores)
-    mates = [c for c in cores if c != core and topo.host(c) == topo.host(core)]
+    base, i = core - core % 8, core % 8
+    mates = [base + (i + s) % 8 for s in range(1, 8)]
     same_die = [c for c in mates if topo.die(c) == topo.die(core)]
-    other_die = [c for c in mates if topo.die(c) != topo.die(core)]
+    other_die = [base + (i // 4 * 4 + 4) % 8 + (i + s) % 4 for s in range(4)]
     peer = [c for c in cores if topo.host(c) != topo.host(core) and c % 8 == core % 8][0]
     prank = T.rank_of(peer)
 

@@ -3,7 +3,7 @@ from concourse.bass import DstId, RemoteDMATransfer
 SCRATCH = {
     "land": ("sbuf", [128, 1024], "float32"),
 }
-SEMAPHORES = ["loaded", "sent", "near", "peer", "far", "stored"]
+SEMAPHORES = ["loaded", "sent", "near", "peer", "far_a", "far_b", "stored"]
 
 W = 64
 
@@ -53,17 +53,28 @@ def rank_program(g, core, T, topo):
     g.wait_ge(T.sem.peer, 8)
     g.remote_dma_fused(
         [
-            RemoteDMATransfer(dst_ids=ids(mates), dma_engine_mask=0xFFFF, remote_sem=T.sem.far,
-                              srcs=[theirs], dsts=[theirs] * 7),
+            RemoteDMATransfer(dst_ids=ids(other_die), dma_engine_mask=0xFFFF, remote_sem=T.sem.far_a,
+                              srcs=[theirs], dsts=[theirs] * 4),
+        ],
+        local_sem=T.sem.sent,
+    )
+    g.remote_dma_fused(
+        [
+            RemoteDMATransfer(dst_ids=ids(same_die), dma_engine_mask=0xFFFF, remote_sem=T.sem.far_b,
+                              srcs=[theirs], dsts=[theirs] * 3),
         ],
         local_sem=T.sem.sent,
     )
 
     h0 = (rank // 8) * 512
     p0 = 512 - h0
+    b0 = p0 + (i // 4) * 256
+    a0 = p0 + (1 - i // 4) * 256
     g.wait_ge(T.sem.near, 7 * 8)
     g.dma_start(T.y[:, h0:h0 + 512], T.land[:, h0:h0 + 512]).then_inc(T.sem.stored, 16)
-    g.wait_ge(T.sem.far, 7 * 16)
-    g.dma_start(T.y[:, p0:p0 + 512], T.land[:, p0:p0 + 512]).then_inc(T.sem.stored, 16)
-    g.wait_ge(T.sem.sent, 16 + 8 + 16)
-    g.wait_ge(T.sem.stored, 32)
+    g.wait_ge(T.sem.far_a, 4 * 16)
+    g.dma_start(T.y[:, a0:a0 + 256], T.land[:, a0:a0 + 256]).then_inc(T.sem.stored, 16)
+    g.wait_ge(T.sem.far_b, 3 * 16)
+    g.dma_start(T.y[:, b0:b0 + 256], T.land[:, b0:b0 + 256]).then_inc(T.sem.stored, 16)
+    g.wait_ge(T.sem.sent, 16 + 8 + 16 + 16)
+    g.wait_ge(T.sem.stored, 48)

from concourse.bass import DstId, RemoteDMATransfer

SCRATCH = {
    "land": ("sbuf", [128, 1024], "float32"),
}
SEMAPHORES = ["loaded", "sent", "near", "peer", "far_a", "far_b", "stored"]

W = 64


def rank_program(g, core, T, topo):
    rank = T.rank_of(core)
    if rank is None:
        return
    cores = list(T.cores)
    base, i = core - core % 8, core % 8
    mates = [base + (i + s) % 8 for s in range(1, 8)]
    same_die = [c for c in mates if topo.die(c) == topo.die(core)]
    other_die = [base + (i // 4 * 4 + 4) % 8 + (i + s) % 4 for s in range(4)]
    peer = [c for c in cores if topo.host(c) != topo.host(core) and c % 8 == core % 8][0]
    prank = T.rank_of(peer)

    def ids(dsts):
        out = []
        for d in dsts:
            rid, pid = topo.addr(d, core)
            out.append(DstId(rid=rid, pnc=pid))
        return out

    mine = T.land[:, rank * W:(rank + 1) * W]
    theirs = T.land[:, prank * W:(prank + 1) * W]

    g.dma_start(mine, T.x[:]).then_inc(T.sem.loaded, 16)
    g.wait_ge(T.sem.loaded, 16)

    g.remote_dma_fused(
        [
            RemoteDMATransfer(dst_ids=ids([peer]), dma_engine_mask=0x00FF, remote_sem=T.sem.peer,
                              srcs=[mine], dsts=[mine]),
            RemoteDMATransfer(dst_ids=ids(other_die), dma_engine_mask=0xFF00, remote_sem=T.sem.near,
                              srcs=[mine], dsts=[mine] * 4),
        ],
        local_sem=T.sem.sent,
    )
    g.remote_dma_fused(
        [
            RemoteDMATransfer(dst_ids=ids(same_die), dma_engine_mask=0x00FF, remote_sem=T.sem.near,
                              srcs=[mine], dsts=[mine] * 3),
        ],
        local_sem=T.sem.sent,
    )

    g.wait_ge(T.sem.peer, 8)
    g.remote_dma_fused(
        [
            RemoteDMATransfer(dst_ids=ids(other_die), dma_engine_mask=0xFFFF, remote_sem=T.sem.far_a,
                              srcs=[theirs], dsts=[theirs] * 4),
        ],
        local_sem=T.sem.sent,
    )
    g.remote_dma_fused(
        [
            RemoteDMATransfer(dst_ids=ids(same_die), dma_engine_mask=0xFFFF, remote_sem=T.sem.far_b,
                              srcs=[theirs], dsts=[theirs] * 3),
        ],
        local_sem=T.sem.sent,
    )

    h0 = (rank // 8) * 512
    p0 = 512 - h0
    b0 = p0 + (i // 4) * 256
    a0 = p0 + (1 - i // 4) * 256
    g.wait_ge(T.sem.near, 7 * 8)
    g.dma_start(T.y[:, h0:h0 + 512], T.land[:, h0:h0 + 512]).then_inc(T.sem.stored, 16)
    g.wait_ge(T.sem.far_a, 4 * 16)
    g.dma_start(T.y[:, a0:a0 + 256], T.land[:, a0:a0 + 256]).then_inc(T.sem.stored, 16)
    g.wait_ge(T.sem.far_b, 3 * 16)
    g.dma_start(T.y[:, b0:b0 + 256], T.land[:, b0:b0 + 256]).then_inc(T.sem.stored, 16)
    g.wait_ge(T.sem.sent, 16 + 8 + 16 + 16)
    g.wait_ge(T.sem.stored, 48)
